import numpy as np
import ml_dtypes


def mxq(x, axis, fmt="e4m3"):
    dtype, down = {"e4m3": (ml_dtypes.float8_e4m3fn, 7), "e5m2": (ml_dtypes.float8_e5m2, 14)}[fmt]
    v = np.moveaxis(np.asarray(x, np.float32).astype(ml_dtypes.bfloat16).astype(np.float64), axis, -1)
    blocks = v.reshape(v.shape[:-1] + (-1, 32))
    amax = np.abs(blocks).max(-1, keepdims=True)
    byte = np.maximum(np.where(amax > 0, np.frexp(amax)[1] - 1 + 127, 0) - down, 1)
    scale = np.exp2(byte - 127.0)
    codes = (blocks / scale).astype(np.float32).astype(dtype).astype(np.float64)
    return np.moveaxis((codes * scale).reshape(v.shape), -1, axis)


WIDE = False


def mx_kscale(k):
    if not WIDE:
        return np.ones(k)
    levels = np.array([10, -10, 5, -5, 0])
    if k % 512:
        return np.exp2(np.random.permutation(np.resize(levels, k // 32))).repeat(32)
    a = np.empty((k // 512, 16))
    for p in range(k // 512):
        a[p, :8] = np.random.permutation(np.resize(levels, 8))
        for g in range(8):
            far = levels[np.abs(levels - a[p, g]) >= 10]
            a[p, g + 8] = far[np.random.randint(len(far))]
    return np.exp2(a.ravel()).repeat(32)


BF16 = ml_dtypes.bfloat16


def bf(x):
    return np.asarray(x, np.float32).astype(BF16)


def f64(x):
    return np.asarray(x).astype(np.float64)


E2M1 = np.array([0.0, 0.5, 1.0, 1.5, 2.0, 3.0, 4.0, 6.0, -0.0, -0.5, -1.0, -1.5, -2.0, -3.0, -4.0, -6.0])


def pack_weight(w, fmt):
    k, n = w.shape
    w = f64(bf(w)).reshape(k // 32, 32, n)
    amax = np.abs(w).max(1)
    if fmt == "e4m3":
        byte = np.frexp(amax)[1] - 1 + 127 - 7
    else:
        mant, ex = np.frexp(amax / 6.0)
        byte = np.where(mant > 0.5, ex, ex - 1) + 127
    byte = np.clip(np.where(amax > 0, byte, 1), 1, 254)
    scaled = (w * np.exp2(127.0 - byte)[:, None, :]).reshape(k, n).astype(np.float32)
    by_word = np.ascontiguousarray(scaled.reshape(k // 512, 128, 4, n).transpose(0, 1, 3, 2))
    if fmt == "e4m3":
        words = by_word.astype(ml_dtypes.float8_e4m3fn).view(np.uint8)
    else:
        c = by_word.astype(ml_dtypes.float4_e2m1fn).view(np.uint8) & 0xF
        words = c[..., 0::2] | (c[..., 1::2] << 4)
    return np.ascontiguousarray(words), np.ascontiguousarray(byte.astype(np.uint8).reshape(k // 512, 16, n))


def unpack_weight(words, scales, fmt):
    g, p, n, _ = words.shape
    if fmt == "e4m3":
        vals = np.ascontiguousarray(words).view(ml_dtypes.float8_e4m3fn).astype(np.float64)
    else:
        nib = np.empty((g, p, n, 4), np.uint8)
        nib[..., 0::2] = words & 0xF
        nib[..., 1::2] = words >> 4
        vals = E2M1[nib]
    vals = vals * np.repeat(np.exp2(scales.astype(np.float64) - 127.0), 8, axis=1)[..., None]
    return vals.transpose(0, 1, 3, 2).reshape(g * 512, n)


B, T, D, F, E = 2, 1024, 512, 1024, 1024


def draw0():
    s, t = mx_kscale(D), mx_kscale(T)
    k = bf(np.random.standard_normal((B, T, D)) * s)
    u1_words, u1_scales = pack_weight(np.random.standard_normal((D, F)) / np.sqrt(D) / s[:, None], "e4m3")
    u2_words, u2_scales = pack_weight(np.random.standard_normal((D, F)) / np.sqrt(D) / s[:, None], "e4m3")
    return {
        "k": k,
        "u1_words": u1_words,
        "u1_scales": u1_scales,
        "u2_words": u2_words,
        "u2_scales": u2_scales,
        "g": bf((1.0 + 0.1 * np.random.standard_normal((B, T))) * t),
        "v": bf(np.random.standard_normal((B, T, E)) / np.sqrt(T) / t[:, None]),
        "a": bf(np.random.uniform(0.5, 1.0, F)),
        "s0": bf(np.random.standard_normal((B, F, E))),
    }


def sketch_features(k, u1_words, u1_scales, u2_words, u2_scales, g):
    kq = mxq(f64(k), 2, "e4m3")
    p1 = kq @ unpack_weight(u1_words, u1_scales, "e4m3")
    p2 = kq @ unpack_weight(u2_words, u2_scales, "e4m3")
    return p1 * p2 * f64(g)[:, :, None]


def core(k, u1_words, u1_scales, u2_words, u2_scales, g, v, a, s0):
    phi = sketch_features(k, u1_words, u1_scales, u2_words, u2_scales, g)
    m = mxq(phi, 1, "e4m3").transpose(0, 2, 1) @ mxq(f64(v), 1, "e4m3")
    return f64(a)[None, :, None] * f64(s0) + m


def e4m3fn_bytes(y):
    return np.clip(np.asarray(y, np.float64), -448.0, 448.0).astype(np.float32).astype(ml_dtypes.float8_e4m3fn).view(np.uint8)


def e4m3fn_values(b):
    return np.asarray(b, np.uint8).view(ml_dtypes.float8_e4m3fn).astype(np.float64)


def setup_inputs():
    d = draw0()
    x0 = np.asarray(d['v']).astype(np.float64)
    s = (np.max(np.abs(x0), axis=(0, 2), keepdims=True) / 448.0).astype(np.float32)
    out = {}
    for k, v in d.items():
        if k == 'v':
            out['v_bytes'] = e4m3fn_bytes(x0 / s.astype(np.float64))
            out['v_scale'] = s
        else:
            out[k] = v
    return out


def reference(k, u1_words, u1_scales, u2_words, u2_scales, g, v_bytes, v_scale, a, s0):
    return core(k, u1_words, u1_scales, u2_words, u2_scales, g, e4m3fn_values(v_bytes) * v_scale.astype(np.float64), a, s0)

@@ -1,0 +1,489 @@
+from contextlib import ExitStack
+
+import concourse.mybir as mybir
+from concourse.masks import make_identity
+
+B, T, D, F, E = 2, 1024, 512, 1024, 1024
+
+FLOPS = 2 * B * T * D * F * 2 + 2 * B * T * F * E
+
+F32 = mybir.dt.float32
+BF16 = mybir.dt.bfloat16
+U32 = mybir.dt.uint32
+I32 = mybir.dt.int32
+U8 = mybir.dt.uint8
+FP8 = mybir.dt.float8_e4m3fn
+FP8X4 = mybir.dt.float8_e4m3fn_x4
+
+COPY = mybir.ActivationFunctionType.Copy
+MULT = mybir.AluOpType.mult
+ADD = mybir.AluOpType.add
+
+P = 128
+PACK = 4
+GROUP = P * PACK
+GROUPS = T // GROUP
+HALF = 512
+HALVES = F // HALF
+QUARTERS = HALF // P
+UNITS = B * HALVES * GROUPS
+SLOTS = UNITS * QUARTERS
+OUT_BANKS = B * (F // P) * (E // HALF)
+LEAD = 7
+VA = 6
+VSTEP = 8
+VB = 16
+VSTEPB = 6
+KA = 9
+KB = 15
+OUT_AT = (12, 15, 22, 19, 37, 43, 52, 54)
+MODES = ("v", "v", "v", "s", "s", "s", "s", "s")
+PLANES = (4, 1, 1, 1, 0, 0, 0, 2)
+GM_FIRST = 9
+GM_LAST = 7
+GM_Q = (0,)
+
+
+def tile_tensorsketchkeyvaluestate_w8_kernel(
+    tc, k, u1_words, u1_scales, u2_words, u2_scales, g, v_bytes, v_scale, a, s0, out
+):
+    nc = tc.nc
+    with ExitStack() as ctx:
+        keep = ctx.enter_context(tc.tile_pool(name="keep", bufs=1))
+        work = ctx.enter_context(tc.tile_pool(name="work", bufs=2))
+        psum = ctx.enter_context(tc.psum_pool(name="psum", bufs=2))
+        done = set()
+
+        def first(key):
+            new = key not in done
+            done.add(key)
+            return new
+
+
+        u_scale = []
+        for w in range(2):
+            plane = keep.tile([P, F], U8, name=f"u_scale{w}", align_bytes=64)
+            nc.vector.memset(plane[:].bitcast(I32), 0)
+            u_scale.append(plane)
+        ident = keep.tile([P, P], F32, name="ident")
+        warm = keep.tile([P, 1], F32, name="warm")
+        nc.vector.memset(warm[:], 0.0)
+        warm_out = keep.tile([P, 1], F32, name="warm_out")
+        nc.scalar.activation(out=warm_out[:], in_=warm[:], func=COPY, scale=warm[:])
+        a_pad = keep.tile([P, P], F32, name="a_pad")
+        nc.vector.memset(a_pad[:], 0.0)
+
+        k_rows = {}
+        v_code = {}
+        for b in range(B):
+            for t in range(GROUPS):
+                k_rows[b, t] = keep.tile([P, PACK, D], BF16, name=f"k_rows{b}{t}", align_bytes=64)
+                v_code[b, t] = keep.tile([P, PACK, E], U8, name=f"v_code{b}{t}", align_bytes=64)
+        u_code = keep.tile([P, 2, F], U32, name="u_code", align_bytes=64)
+        s0_rows = [keep.tile([P, F // P, E], BF16, name=f"s0_rows{b}", align_bytes=64) for b in range(B)]
+        v_gain = keep.tile([P, GROUPS, PACK], F32, name="v_gain")
+        g_bf = keep.tile([P, B * GROUPS, PACK], BF16, name="g_bf")
+        a_bf = keep.tile([F // P, P], BF16, name="a_bf")
+
+        def load_k(b, t, lo, hi):
+            rows = k[b].rearrange("(t p j) d -> t p j d", p=P, j=PACK)[t]
+            nc.sync.dma_start(out=k_rows[b, t][:, lo:hi, :], in_=rows[:, lo:hi, :])
+
+        def load_v(b, t, lo, hi):
+            rows = v_bytes[b].rearrange("(t p j) e -> t p j e", p=P, j=PACK)[t]
+            nc.sync.dma_start(out=v_code[b, t][:, lo:hi, :], in_=rows[:, lo:hi, :])
+
+        def load_u(h, w):
+            words = (u1_words, u2_words)[w]
+            src = words.rearrange("o p n t -> p (o n t)")[:, h * HALF * 4:(h + 1) * HALF * 4]
+            nc.sync.dma_start(out=u_code[:, w, h * HALF:(h + 1) * HALF].bitcast(I32), in_=src.bitcast(I32))
+
+        def load_us(w):
+            scales = (u1_scales, u2_scales)[w]
+            for q in range(4):
+                nc.sync.dma_start(
+                    out=u_scale[w][32 * q:32 * q + 4, :].bitcast(I32),
+                    in_=scales[0, 4 * q:4 * q + 4, :].bitcast(I32),
+                )
+
+        def load_s0(b, lo, hi):
+            rows = s0[b].rearrange("(c p) e -> p c e", p=P)
+            nc.sync.dma_start(out=s0_rows[b][:, lo:hi, :], in_=rows[:, lo:hi, :])
+
+        nc.gpsimd.dma_start(out=v_gain[:], in_=v_scale.rearrange("o (t p j) x -> p (o t) (j x)", p=P, j=PACK))
+        make_identity(nc, ident[:])
+        nc.gpsimd.dma_start(out=g_bf[:], in_=g.rearrange("b (t p j) -> p (b t) j", p=P, j=PACK))
+        nc.gpsimd.dma_start(out=a_bf[:], in_=a.rearrange("(c p) -> c p", p=P))
+        load_k(0, 0, 0, 2)
+        load_us(0)
+        load_u(0, 0)
+        load_k(0, 0, 2, 4)
+        load_v(0, 0, 0, 4)
+        load_us(1)
+        load_u(0, 1)
+        load_k(0, 1, 0, 4)
+        load_v(0, 1, 0, 4)
+        load_u(1, 0)
+        load_u(1, 1)
+        load_k(1, 0, 0, 4)
+        load_s0(0, 0, 4)
+        load_v(1, 0, 0, 4)
+        load_k(1, 1, 0, 4)
+        load_v(1, 1, 0, 4)
+        load_s0(0, 4, 8)
+        load_s0(1, 0, 4)
+        load_s0(1, 4, 8)
+
+        ident_bf = keep.tile([P, P], BF16, name="ident_bf")
+        nc.vector.tensor_copy(out=ident_bf[:], in_=ident[:])
+        g_f32 = keep.tile([P, B * GROUPS, PACK], F32, name="g_f32")
+        a_f32 = keep.tile([P, F // P], F32, name="a_f32")
+
+        k_quad = {}
+        kq = {}
+        kq_s = {}
+        xt = {}
+
+        def k_transpose(b, t, half):
+            if not first(("kt", b, t, half)):
+                return
+            bank = psum.tile([P, 2, 2, P], F32, name="bank_o", bufs=4)
+            words = k_rows[b, t][:].rearrange("p j d -> p (j d)").bitcast(F32)
+            for jj in range(2):
+                j0 = (2 * half + jj) * (D // 2)
+                for u in range(2):
+                    nc.tensor.transpose(bank[:, jj, u, :], words[:, j0 + u:j0 + D // 2:2], ident[:])
+            xt[b, t, half] = bank
+
+        def k_copy(b, t, half, engine):
+            if not first(("kc", b, t, half)):
+                return
+            k_transpose(b, t, half)
+            if half == 1:
+                k_copy(b, t, 0, engine)
+            if half == 0:
+                k_quad[b, t] = work.tile([P, GROUP * PACK], BF16, name="k_quad", align_bytes=64)
+                kq[b, t] = keep.tile([P, GROUP], U32, name=f"kq{b}{t}", align_bytes=64)
+                kq_s[b, t] = keep.tile([P, GROUP], U8, name=f"kqs{b}{t}", align_bytes=64)
+            width = GROUP * PACK // 2
+            dst = k_quad[b, t][:, half * width:(half + 1) * width].bitcast(F32)
+            dst = dst.rearrange("p (j m u) -> p j m u", j=2, u=2)
+            srcv = xt[b, t, half][:].rearrange("p j u m -> p j m u")
+            if engine == "v":
+                nc.vector.tensor_copy(out=dst, in_=srcv)
+            else:
+                nc.scalar.copy(out=dst, in_=srcv)
+
+        def k_quantize(b, t, half):
+            if not first(("kq", b, t, half)):
+                return
+            k_copy(b, t, half, "s")
+            width = GROUP // 2
+            cols = slice(half * width, (half + 1) * width)
+            nc.vector.quantize_mx(
+                out=kq[b, t][:, cols].bitcast(FP8X4),
+                scales=kq_s[b, t][:, cols],
+                in_=k_quad[b, t][:, half * width * 4:(half + 1) * width * 4],
+            )
+
+        pieces = [(b, t, eh) for b in range(B) for eh in range(2) for t in range(GROUPS)]
+        v_wide = {}
+        v_quad = {}
+        turned = {}
+        vq = {}
+        vq_s = {}
+
+        def v_widen(b, t, eh, j, engine):
+            if not first(("vw", b, t, eh, j)):
+                return
+            if j > 0:
+                v_widen(b, t, eh, 0, plane_engine(b, t, eh, 0))
+            if j == 0:
+                v_wide[b, t, eh] = work.tile([P, PACK, HALF], BF16, name="v_wide", align_bytes=64, bufs=4)
+            dst = v_wide[b, t, eh][:, j, :]
+            srcv = v_code[b, t][:, j, eh * HALF:(eh + 1) * HALF].bitcast(FP8)
+            gain = v_gain[:, t, j:j + 1]
+            if engine == "v":
+                nc.vector.tensor_scalar(out=dst, in0=srcv, scalar1=gain, scalar2=None, op0=MULT)
+            else:
+                nc.scalar.activation(out=dst, in_=srcv, func=COPY, scale=gain)
+
+        def plane_engine(b, t, eh, j):
+            return "s" if j < PACK - PLANES[pieces.index((b, t, eh))] else "v"
+
+        def v_lay(b, t, eh):
+            by = MODES[pieces.index((b, t, eh))]
+            if by == "ps" or by == "pv":
+                for half in range(2):
+                    v_exit(b, t, eh, half, by[1])
+            else:
+                parts = 4 if by != "v" else 1
+                for part in range(parts):
+                    v_interleave(b, t, eh, by, part, parts)
+
+        def v_interleave(b, t, eh, engine, part, parts):
+            if not first(("vi", b, t, eh, part)):
+                return
+            for j in range(PACK):
+                v_widen(b, t, eh, j, plane_engine(b, t, eh, j))
+            if part > 0:
+                v_interleave(b, t, eh, engine, part - 1, parts)
+            if part == 0:
+                v_quad[b, t, eh] = work.tile([P, HALF, PACK], BF16, name="v_quad", align_bytes=64, bufs=3)
+            cols = slice(part * HALF // parts, (part + 1) * HALF // parts)
+            dst = v_quad[b, t, eh][:, cols, :].rearrange("p (c i) t -> p c t i", i=4)
+            srcv = v_wide[b, t, eh][:, :, cols].rearrange("p t (c i) -> p c t i", i=4)
+            if engine == "v":
+                nc.vector.tensor_copy(out=dst, in_=srcv)
+            elif engine == "g":
+                nc.gpsimd.tensor_scalar(out=dst, in0=srcv, scalar1=1.0, scalar2=0.0, op0=MULT, op1=ADD)
+            else:
+                nc.scalar.copy(out=dst, in_=srcv)
+
+        def v_turn(b, t, eh, half):
+            if not first(("vt", b, t, eh, half)):
+                return
+            for j in range(PACK):
+                v_widen(b, t, eh, j, plane_engine(b, t, eh, j))
+            bank = psum.tile([P, HALF // 2, PACK], BF16, name="bank_o", bufs=4)
+            for x in range(2):
+                cols = slice(half * HALF // 2 + x * P, half * HALF // 2 + (x + 1) * P)
+                nc.tensor.matmul(
+                    out=bank[:, x * P:(x + 1) * P, :],
+                    lhsT=ident_bf[:],
+                    rhs=v_wide[b, t, eh][:, :, cols].rearrange("p t n -> p n t"),
+                    start=True,
+                    stop=True,
+                )
+            turned[b, t, eh, half] = bank
+
+        def v_exit(b, t, eh, half, engine):
+            if not first(("vx", b, t, eh, half)):
+                return
+            if half == 1:
+                v_exit(b, t, eh, 0, engine)
+            v_turn(b, t, eh, half)
+            if half == 0:
+                v_quad[b, t, eh] = work.tile([P, HALF, PACK], BF16, name="v_quad", align_bytes=64, bufs=3)
+            dst = v_quad[b, t, eh][:, half * HALF // 2:(half + 1) * HALF // 2, :]
+            if engine == "v":
+                nc.vector.tensor_copy(out=dst, in_=turned[b, t, eh, half][:])
+            else:
+                nc.scalar.copy(out=dst, in_=turned[b, t, eh, half][:])
+
+        def v_quantize(b, t, eh):
+            if not first(("vq", b, t, eh)):
+                return
+            v_lay(b, t, eh)
+            vq[b, t, eh] = keep.tile([P, HALF], U32, name=f"vq{b}{t}{eh}", align_bytes=64)
+            vq_s[b, t, eh] = keep.tile([P, HALF], U8, name=f"vqs{b}{t}{eh}", align_bytes=64)
+            nc.vector.quantize_mx(
+                out=vq[b, t, eh][:].bitcast(FP8X4),
+                scales=vq_s[b, t, eh][:],
+                in_=v_quad[b, t, eh][:].rearrange("p n t -> p (n t)"),
+            )
+
+        units = [(b, h, t) for b in range(B) for h in range(HALVES) for t in range(GROUPS)]
+        p1_bank = {}
+        p1_sb = {}
+        p2_bank = {}
+        phi = {}
+        pq = {}
+        pq_s = {}
+
+        def p1_matmul(i, j):
+            if not first(("p1", i, j)):
+                return
+            k_quantize(units[i][0], units[i][2], j // 2)
+            b, h, t = units[i]
+            bank = psum.tile([P, HALF], F32, name="bank_p1", bufs=2)
+            nc.tensor.matmul_mx(
+                out=bank[:],
+                lhsT=kq[b, t][:, j * P:(j + 1) * P].bitcast(FP8X4),
+                lhsT_scale=kq_s[b, t][:, j * P:(j + 1) * P],
+                rhs=u_code[:, 0, h * HALF:(h + 1) * HALF].bitcast(FP8X4),
+                rhs_scale=u_scale[0][:, h * HALF:(h + 1) * HALF],
+                start=True,
+                stop=True,
+            )
+            p1_bank[i, j] = bank
+
+        def p1_gain(i, j):
+            if not first(("p1g", i, j)):
+                return
+            if j > 0:
+                p1_gain(i, j - 1)
+            p1_matmul(i, j)
+            b, h, t = units[i]
+            if j == 0:
+                p1_sb[i] = work.tile([P, PACK, HALF], F32, name="p1_sb", bufs=3)
+            nc.scalar.activation(
+                out=p1_sb[i][:, j, :], in_=p1_bank[i, j][:], func=COPY,
+                scale=g_f32[:, b * GROUPS + t, j:j + 1],
+            )
+
+        def p2_matmul(i, q):
+            if not first(("p2", i, q)):
+                return
+            for half in range(2):
+                k_quantize(units[i][0], units[i][2], half)
+            b, h, t = units[i]
+            bank = psum.tile([P, PACK, P], F32, name="bank_p2", bufs=2)
+            f0 = h * HALF + q * P
+            for j in range(PACK):
+                nc.tensor.matmul_mx(
+                    out=bank[:, j, :],
+                    lhsT=kq[b, t][:, j * P:(j + 1) * P].bitcast(FP8X4),
+                    lhsT_scale=kq_s[b, t][:, j * P:(j + 1) * P],
+                    rhs=u_code[:, 1, f0:f0 + P].bitcast(FP8X4),
+                    rhs_scale=u_scale[1][:, f0:f0 + P],
+                    start=True,
+                    stop=True,
+                )
+            p2_bank[i, q] = bank
+
+        def phi_mult(i, q):
+            if not first(("phi", i, q)):
+                return
+            for j in range(PACK):
+                p1_gain(i, j)
+            p2_matmul(i, q)
+            if q == 0:
+                phi[i] = work.tile([P, HALF, PACK], BF16, name="phi", align_bytes=64, bufs=3)
+            cols = slice(q * P, (q + 1) * P)
+            nc.vector.tensor_tensor(
+                out=phi[i][:, cols, :].rearrange("p (c i) t -> p c t i", i=2),
+                in0=p2_bank[i, q][:].rearrange("p t (c i) -> p c t i", i=2),
+                in1=p1_sb[i][:, :, cols].rearrange("p t (c i) -> p c t i", i=2),
+                op=MULT,
+            )
+
+        def phi_mult_g(i, q):
+            if not first(("phi", i, q)):
+                return
+            for j in range(PACK):
+                p1_gain(i, j)
+            p2_matmul(i, q)
+            if q == 0:
+                phi[i] = work.tile([P, HALF, PACK], BF16, name="phi", align_bytes=64, bufs=3)
+            p2_sb = work.tile([P, PACK, P], F32, name="p2_sb", bufs=2)
+            nc.scalar.copy(out=p2_sb[:], in_=p2_bank[i, q][:])
+            cols = slice(q * P, (q + 1) * P)
+            nc.gpsimd.tensor_tensor(
+                out=phi[i][:, cols, :].rearrange("p (c i) t -> p c t i", i=4),
+                in0=p2_sb[:].rearrange("p t (c i) -> p c t i", i=4),
+                in1=p1_sb[i][:, :, cols].rearrange("p t (c i) -> p c t i", i=4),
+                op=MULT,
+            )
+
+        def phi_quantize(i):
+            if not first(("pq", i)):
+                return
+            pq[i] = keep.tile([P, HALF], U32, name=f"pq{i}", align_bytes=64)
+            pq_s[i] = keep.tile([P, HALF], U8, name=f"pqs{i}", align_bytes=64)
+            nc.vector.quantize_mx(
+                out=pq[i][:].bitcast(FP8X4),
+                scales=pq_s[i][:],
+                in_=phi[i][:].rearrange("p n t -> p (n t)"),
+            )
+
+        out_bank = {}
+
+        def place(n):
+            b, rest = divmod(n, OUT_BANKS // B)
+            outer, ft = divmod(rest, QUARTERS)
+            h, eh = divmod(outer, 2) if b < B - 1 else (outer % 2, outer // 2)
+            return b, h * QUARTERS + ft, eh
+
+        def out_matmul(n):
+            b, c, eh = place(n)
+            h, ft = divmod(c, QUARTERS)
+            for t in range(GROUPS):
+                phi_quantize((b * HALVES + h) * GROUPS + t)
+                v_quantize(b, t, eh)
+            bank = psum.tile([P, HALF], F32, name="bank_o", bufs=4)
+            for t in range(GROUPS):
+                i = (b * HALVES + h) * GROUPS + t
+                nc.tensor.matmul_mx(
+                    out=bank[:],
+                    lhsT=pq[i][:, ft * P:(ft + 1) * P].bitcast(FP8X4),
+                    lhsT_scale=pq_s[i][:, ft * P:(ft + 1) * P],
+                    rhs=vq[b, t, eh][:].bitcast(FP8X4),
+                    rhs_scale=vq_s[b, t, eh][:],
+                    start=(t == 0),
+                    stop=(t == GROUPS - 1),
+                )
+            out_bank[n] = bank
+
+        def out_sum(n):
+            b, c, eh = place(n)
+            total = work.tile([P, HALF], F32, name="out_sb", bufs=6)
+            cols = slice(eh * HALF, (eh + 1) * HALF)
+            nc.vector.scalar_tensor_tensor(
+                out=total[:], in0=s0_rows[b][:, c, cols], scalar=a_f32[:, c:c + 1],
+                in1=out_bank[n][:], op0=MULT, op1=ADD,
+            )
+            nc.sync.dma_start(out=out[b, c * P:(c + 1) * P, cols], in_=total[:])
+
+        def a_columns():
+            nc.scalar.copy(out=a_pad[0:F // P, :], in_=a_bf[:])
+            bank = psum.tile([P, P], F32, name="bank_o", bufs=4)
+            nc.tensor.transpose(bank[:], a_pad[:], ident[:])
+            nc.scalar.copy(out=a_f32[:], in_=bank[:, 0:F // P])
+
+        k_transpose(0, 0, 0)
+        k_transpose(0, 0, 1)
+        k_copy(0, 0, 0, "v")
+        nc.vector.tensor_copy(out=g_f32[:], in_=g_bf[:])
+        k_copy(0, 0, 1, "s")
+        k_quantize(0, 0, 0)
+        k_quantize(0, 0, 1)
+        for j in range(PACK):
+            p1_gain(0, j)
+        p2_matmul(0, 0)
+        p2_matmul(0, 1)
+        k_transpose(0, 1, 0)
+        k_transpose(0, 1, 1)
+        v_lay(*pieces[0])
+        k_quantize(0, 1, 0)
+        k_quantize(0, 1, 1)
+
+        for s in range(SLOTS + OUT_BANKS):
+            i, q = divmod(s, QUARTERS)
+            if s < SLOTS:
+                (phi_mult_g if GM_FIRST <= i < GM_LAST and q in GM_Q else phi_mult)(i, q)
+            if q == 1 and 0 < i <= UNITS:
+                phi_quantize(i - 1)
+            if s == 1:
+                v_quantize(*pieces[0])
+                a_columns()
+            if s + 2 < SLOTS:
+                p2_matmul((s + 2) // QUARTERS, (s + 2) % QUARTERS)
+            for x in range(QUARTERS, min(s + LEAD + 1, SLOTS)):
+                p1_gain(x // QUARTERS, x % QUARTERS)
+            for t, at in ((0, KA), (1, KB)):
+                if s == at:
+                    k_transpose(1, t, 0)
+                    k_transpose(1, t, 1)
+                if s == at + 1:
+                    k_copy(1, t, 0, "s")
+                    k_copy(1, t, 1, "s")
+                if s == at + 2:
+                    k_quantize(1, t, 0)
+                    k_quantize(1, t, 1)
+            for m in range(1, 8):
+                at, step = (VA + VSTEP * (m - 1), VSTEP) if m < 4 else (VB + VSTEPB * (m - 4), VSTEPB)
+                b, t, eh = pieces[m]
+                for j in range(PACK):
+                    if s == at + j * step // PACK:
+                        v_widen(b, t, eh, j, plane_engine(b, t, eh, j))
+                if s == at + step:
+                    v_lay(b, t, eh)
+                if s == at + step + 1:
+                    v_quantize(b, t, eh)
+            for o in range(8):
+                for x in range(QUARTERS):
+                    if s == OUT_AT[o] + x - 2:
+                        out_matmul(o * QUARTERS + x)
+                    if s == OUT_AT[o] + x:
+                        out_sum(o * QUARTERS + x)

@@ -29,19 +29,62 @@ QUARTERS = HALF // P
 UNITS = B * HALVES * GROUPS
 SLOTS = UNITS * QUARTERS
 OUT_BANKS = B * (F // P) * (E // HALF)
-LEAD = 7
-VA = 6
-VSTEP = 8
-VB = 16
-VSTEPB = 6
-KA = 9
-KB = 15
-OUT_AT = (12, 15, 22, 19, 37, 43, 52, 54)
-MODES = ("v", "v", "v", "s", "s", "s", "s", "s")
-PLANES = (4, 1, 1, 1, 0, 0, 0, 2)
-GM_FIRST = 9
-GM_LAST = 7
-GM_Q = (0,)
+
+LEAD = 6
+W_AT = (8, 0, 8, 14)
+W_STEP = (3, 2, 2, 2)
+I_STEP = 2
+KA = 6
+KB = 10
+OUT_AT = (14, 19, 21, 27, 40, 41, 45, 55)
+MODES = ("v", "v", "v", "g", "g", "g", "g", "s")
+PLANES = (3, 1, 0, 0)
+GMASK = (0, 4, 0, 0, 8, 8, 8, 10)
+LAG = 90
+PORT = 1
+
+DEPTH = {"p1": 2, "p2": 2, "o": 4, "p1_sb": 3, "p2_sb": 2, "phi": 3, "k_quad": 2, "v_wide": 2, "v_quad": 3, "out_sb": 4}
+
+
+def issue_in_start_order(tasks):
+    free, finish, freed, readers, tenants = {}, {}, {}, {}, {}
+    for name, engine, weight, needs, takes, frees, issue in tasks:
+        for tile in frees:
+            readers[tile] = readers.get(tile, 0) + 1
+    waiting = list(tasks)
+    while waiting:
+        best = None
+        for task in waiting:
+            name, engine, weight, needs, takes, frees, issue = task
+            if not all([n in finish for n in needs]):
+                continue
+            port = engine == "g" or engine == "v" and name[0] in ("kq", "vq", "pq", "w", "lay")
+            start = max([free.get(engine, 0)] + [finish[n] for n in needs])
+            if port and PORT:
+                start = max(start, free.get("port", 0))
+            if takes is not None:
+                held = tenants.setdefault(takes, [])
+                if len(held) >= DEPTH[takes]:
+                    old = held[len(held) - DEPTH[takes]]
+                    if readers.get(old, 0) > 0:
+                        continue
+                    start = max(start, freed[old])
+            if best is None or start < best[0]:
+                best = (start, task)
+        start, task = best
+        name, engine, weight, needs, takes, frees, issue = task
+        waiting.remove(task)
+        issue()
+        free[engine] = start + weight
+        if engine == "g" or engine == "v" and name[0] in ("kq", "vq", "pq", "w", "lay"):
+            free["port"] = start + weight
+        lag = {"load": 1900, "store": 2000, "tile": 0}.get(engine, LAG)
+        finish[name] = start + weight + lag
+        if takes is not None:
+            tenants[takes].append(name)
+        for tile in frees:
+            readers[tile] = readers[tile] - 1
+            freed[tile] = max(freed.get(tile, 0), finish[name])
 
 
 def tile_tensorsketchkeyvaluestate_w8_kernel(
@@ -52,13 +95,12 @@ def tile_tensorsketchkeyvaluestate_w8_kernel(
         keep = ctx.enter_context(tc.tile_pool(name="keep", bufs=1))
         work = ctx.enter_context(tc.tile_pool(name="work", bufs=2))
         psum = ctx.enter_context(tc.psum_pool(name="psum", bufs=2))
-        done = set()
+        ctx.enter_context(tc.manual_schedule())
 
-        def first(key):
-            new = key not in done
-            done.add(key)
-            return new
+        tasks = []
 
+        def add(slot, name, engine, weight, needs, issue, takes=None, frees=()):
+            tasks.append((slot, len(tasks), (name, engine, weight, needs, takes, frees, issue)))
 
         u_scale = []
         for w in range(2):
@@ -66,10 +108,10 @@ def tile_tensorsketchkeyvaluestate_w8_kernel(
             nc.vector.memset(plane[:].bitcast(I32), 0)
             u_scale.append(plane)
         ident = keep.tile([P, P], F32, name="ident")
+        make_identity(nc, ident[:])
         warm = keep.tile([P, 1], F32, name="warm")
         nc.vector.memset(warm[:], 0.0)
         warm_out = keep.tile([P, 1], F32, name="warm_out")
-        nc.scalar.activation(out=warm_out[:], in_=warm[:], func=COPY, scale=warm[:])
         a_pad = keep.tile([P, P], F32, name="a_pad")
         nc.vector.memset(a_pad[:], 0.0)
 
@@ -84,19 +126,21 @@ def tile_tensorsketchkeyvaluestate_w8_kernel(
         v_gain = keep.tile([P, GROUPS, PACK], F32, name="v_gain")
         g_bf = keep.tile([P, B * GROUPS, PACK], BF16, name="g_bf")
         a_bf = keep.tile([F // P, P], BF16, name="a_bf")
+        g_f32 = keep.tile([P, B * GROUPS, PACK], F32, name="g_f32")
+        a_f32 = keep.tile([P, F // P], F32, name="a_f32")
 
         def load_k(b, t, lo, hi):
             rows = k[b].rearrange("(t p j) d -> t p j d", p=P, j=PACK)[t]
             nc.sync.dma_start(out=k_rows[b, t][:, lo:hi, :], in_=rows[:, lo:hi, :])
 
-        def load_v(b, t, lo, hi):
+        def load_v(b, t):
             rows = v_bytes[b].rearrange("(t p j) e -> t p j e", p=P, j=PACK)[t]
-            nc.sync.dma_start(out=v_code[b, t][:, lo:hi, :], in_=rows[:, lo:hi, :])
+            nc.sync.dma_start(out=v_code[b, t][:], in_=rows)
 
         def load_u(h, w):
-            words = (u1_words, u2_words)[w]
-            src = words.rearrange("o p n t -> p (o n t)")[:, h * HALF * 4:(h + 1) * HALF * 4]
-            nc.sync.dma_start(out=u_code[:, w, h * HALF:(h + 1) * HALF].bitcast(I32), in_=src.bitcast(I32))
+            words = (u1_words, u2_words)[w].rearrange("o p n t -> p (o n t)")
+            cols = slice(h * HALF * PACK, (h + 1) * HALF * PACK)
+            nc.sync.dma_start(out=u_code[:, w, h * HALF:(h + 1) * HALF].bitcast(I32), in_=words[:, cols].bitcast(I32))
 
         def load_us(w):
             scales = (u1_scales, u2_scales)[w]
@@ -106,133 +150,127 @@ def tile_tensorsketchkeyvaluestate_w8_kernel(
                     in_=scales[0, 4 * q:4 * q + 4, :].bitcast(I32),
                 )
 
-        def load_s0(b, lo, hi):
+        def load_s0(b, half):
             rows = s0[b].rearrange("(c p) e -> p c e", p=P)
-            nc.sync.dma_start(out=s0_rows[b][:, lo:hi, :], in_=rows[:, lo:hi, :])
+            chunk = slice(half * QUARTERS, (half + 1) * QUARTERS)
+            nc.sync.dma_start(out=s0_rows[b][:, chunk, :], in_=rows[:, chunk, :])
 
-        nc.gpsimd.dma_start(out=v_gain[:], in_=v_scale.rearrange("o (t p j) x -> p (o t) (j x)", p=P, j=PACK))
-        make_identity(nc, ident[:])
-        nc.gpsimd.dma_start(out=g_bf[:], in_=g.rearrange("b (t p j) -> p (b t) j", p=P, j=PACK))
-        nc.gpsimd.dma_start(out=a_bf[:], in_=a.rearrange("(c p) -> c p", p=P))
-        load_k(0, 0, 0, 2)
-        load_us(0)
-        load_u(0, 0)
-        load_k(0, 0, 2, 4)
-        load_v(0, 0, 0, 4)
-        load_us(1)
-        load_u(0, 1)
-        load_k(0, 1, 0, 4)
-        load_v(0, 1, 0, 4)
-        load_u(1, 0)
-        load_u(1, 1)
-        load_k(1, 0, 0, 4)
-        load_s0(0, 0, 4)
-        load_v(1, 0, 0, 4)
-        load_k(1, 1, 0, 4)
-        load_v(1, 1, 0, 4)
-        load_s0(0, 4, 8)
-        load_s0(1, 0, 4)
-        load_s0(1, 4, 8)
+        def load_v_gain():
+            nc.scalar.dma_start(out=v_gain[:], in_=v_scale.rearrange("o (t p j) x -> p (o t) (j x)", p=P, j=PACK))
 
-        ident_bf = keep.tile([P, P], BF16, name="ident_bf")
-        nc.vector.tensor_copy(out=ident_bf[:], in_=ident[:])
-        g_f32 = keep.tile([P, B * GROUPS, PACK], F32, name="g_f32")
-        a_f32 = keep.tile([P, F // P], F32, name="a_f32")
+        def load_g():
+            nc.scalar.dma_start(out=g_bf[:], in_=g.rearrange("b (t p j) -> p (b t) j", p=P, j=PACK))
 
+        def load_a():
+            nc.scalar.dma_start(out=a_bf[:], in_=a.rearrange("(c p) -> c p", p=P))
+
+        def load(name, weight, issue):
+            add(-100, ("load",) + name, "load", weight, (), issue)
+
+        load(("v_gain",), 30, load_v_gain)
+        load(("k", 0, 0, 0), 440, lambda: load_k(0, 0, 0, 2))
+        load(("us", 0), 300, lambda: load_us(0))
+        load(("k", 0, 0, 1), 440, lambda: load_k(0, 0, 2, 4))
+        load(("v", 0, 0), 870, lambda: load_v(0, 0))
+        load(("u", 0, 0), 440, lambda: load_u(0, 0))
+        load(("us", 1), 300, lambda: load_us(1))
+        load(("g",), 30, load_g)
+        load(("u", 0, 1), 440, lambda: load_u(0, 1))
+        load(("k", 0, 1), 870, lambda: load_k(0, 1, 0, 4))
+        load(("v", 0, 1), 870, lambda: load_v(0, 1))
+        load(("u", 1, 0), 440, lambda: load_u(1, 0))
+        load(("u", 1, 1), 440, lambda: load_u(1, 1))
+        load(("a",), 30, load_a)
+        load(("k", 1, 0), 870, lambda: load_k(1, 0, 0, 4))
+        load(("s0", 0, 0), 1750, lambda: load_s0(0, 0))
+        load(("v", 1, 0), 870, lambda: load_v(1, 0))
+        load(("k", 1, 1), 870, lambda: load_k(1, 1, 0, 4))
+        load(("v", 1, 1), 870, lambda: load_v(1, 1))
+        load(("s0", 0, 1), 1750, lambda: load_s0(0, 1))
+        load(("s0", 1, 0), 1750, lambda: load_s0(1, 0))
+        load(("s0", 1, 1), 1750, lambda: load_s0(1, 1))
+
+        nc.scalar.activation(out=warm_out[:], in_=warm[:], func=COPY, scale=warm[:])
+        add(-1, ("g_f32",), "v", 70, (("load", "g"),), lambda: nc.vector.tensor_copy(out=g_f32[:], in_=g_bf[:]))
+
+        banks = {}
         k_quad = {}
         kq = {}
         kq_s = {}
-        xt = {}
 
         def k_transpose(b, t, half):
-            if not first(("kt", b, t, half)):
-                return
-            bank = psum.tile([P, 2, 2, P], F32, name="bank_o", bufs=4)
+            bank = psum.tile([P, 2, 2, P], F32, name="bank_o", bufs=DEPTH["o"])
             words = k_rows[b, t][:].rearrange("p j d -> p (j d)").bitcast(F32)
             for jj in range(2):
                 j0 = (2 * half + jj) * (D // 2)
                 for u in range(2):
                     nc.tensor.transpose(bank[:, jj, u, :], words[:, j0 + u:j0 + D // 2:2], ident[:])
-            xt[b, t, half] = bank
+            banks["kt", b, t, half] = bank
+
+        def k_tiles(b, t):
+            k_quad[b, t] = work.tile([P, GROUP * PACK], BF16, name="k_quad", align_bytes=64, bufs=DEPTH["k_quad"])
+            kq[b, t] = keep.tile([P, GROUP], U32, name=f"kq{b}{t}", align_bytes=64)
+            kq_s[b, t] = keep.tile([P, GROUP], U8, name=f"kqs{b}{t}", align_bytes=64)
 
         def k_copy(b, t, half, engine):
-            if not first(("kc", b, t, half)):
-                return
-            k_transpose(b, t, half)
-            if half == 1:
-                k_copy(b, t, 0, engine)
-            if half == 0:
-                k_quad[b, t] = work.tile([P, GROUP * PACK], BF16, name="k_quad", align_bytes=64)
-                kq[b, t] = keep.tile([P, GROUP], U32, name=f"kq{b}{t}", align_bytes=64)
-                kq_s[b, t] = keep.tile([P, GROUP], U8, name=f"kqs{b}{t}", align_bytes=64)
             width = GROUP * PACK // 2
             dst = k_quad[b, t][:, half * width:(half + 1) * width].bitcast(F32)
             dst = dst.rearrange("p (j m u) -> p j m u", j=2, u=2)
-            srcv = xt[b, t, half][:].rearrange("p j u m -> p j m u")
+            srcv = banks["kt", b, t, half][:].rearrange("p j u m -> p j m u")
             if engine == "v":
                 nc.vector.tensor_copy(out=dst, in_=srcv)
             else:
                 nc.scalar.copy(out=dst, in_=srcv)
 
-        def k_quantize(b, t, half):
-            if not first(("kq", b, t, half)):
-                return
-            k_copy(b, t, half, "s")
-            width = GROUP // 2
-            cols = slice(half * width, (half + 1) * width)
+        def k_quantize(b, t, lo, hi):
             nc.vector.quantize_mx(
-                out=kq[b, t][:, cols].bitcast(FP8X4),
-                scales=kq_s[b, t][:, cols],
-                in_=k_quad[b, t][:, half * width * 4:(half + 1) * width * 4],
+                out=kq[b, t][:, lo:hi].bitcast(FP8X4),
+                scales=kq_s[b, t][:, lo:hi],
+                in_=k_quad[b, t][:, lo * PACK:hi * PACK],
             )
 
-        pieces = [(b, t, eh) for b in range(B) for eh in range(2) for t in range(GROUPS)]
+        def add_k(slot, b, t):
+            add(slot, ("k_tiles", b, t), "tile", 0, (), lambda: k_tiles(b, t), takes="k_quad")
+            for half in range(2):
+                source = ("load", "k", b, t) + ((half,) if (b, t) == (0, 0) else ())
+                engine = "v" if (b, t, half) == (0, 0, 0) else "s"
+                add(slot, ("kt", b, t, half), "t", 420, (source,), lambda half=half: k_transpose(b, t, half), takes="o")
+                add(slot, ("kc", b, t, half), engine, 490, (("kt", b, t, half), ("k_tiles", b, t)),
+                    lambda half=half, engine=engine: k_copy(b, t, half, engine), frees=(("kt", b, t, half),))
+                if (b, t) == (0, 0):
+                    add(slot, ("kq", b, t, half), "v", 290, (("kc", b, t, half),),
+                        lambda half=half: k_quantize(b, t, half * 256, half * 256 + 256), frees=(("k_tiles", b, t),))
+            if (b, t) != (0, 0):
+                add(slot, ("kq", b, t, 0), "v", 510, (("kc", b, t, 0), ("kc", b, t, 1)),
+                    lambda: k_quantize(b, t, 0, GROUP), frees=(("k_tiles", b, t),))
+
+        def k_ready(b, t):
+            return (("kq", b, t, 0), ("kq", b, t, 1)) if (b, t) == (0, 0) else (("kq", b, t, 0),)
+
         v_wide = {}
         v_quad = {}
-        turned = {}
         vq = {}
         vq_s = {}
 
-        def v_widen(b, t, eh, j, engine):
-            if not first(("vw", b, t, eh, j)):
-                return
-            if j > 0:
-                v_widen(b, t, eh, 0, plane_engine(b, t, eh, 0))
-            if j == 0:
-                v_wide[b, t, eh] = work.tile([P, PACK, HALF], BF16, name="v_wide", align_bytes=64, bufs=4)
-            dst = v_wide[b, t, eh][:, j, :]
-            srcv = v_code[b, t][:, j, eh * HALF:(eh + 1) * HALF].bitcast(FP8)
+        def wide_tile(b, t):
+            v_wide[b, t] = work.tile([P, PACK, E], BF16, name="v_wide", align_bytes=64, bufs=DEPTH["v_wide"])
+
+        def v_widen(b, t, j, engine):
+            srcv = v_code[b, t][:, j, :].bitcast(FP8)
             gain = v_gain[:, t, j:j + 1]
             if engine == "v":
-                nc.vector.tensor_scalar(out=dst, in0=srcv, scalar1=gain, scalar2=None, op0=MULT)
+                nc.vector.tensor_scalar(out=v_wide[b, t][:, j, :], in0=srcv, scalar1=gain, scalar2=None, op0=MULT)
             else:
-                nc.scalar.activation(out=dst, in_=srcv, func=COPY, scale=gain)
+                nc.scalar.activation(out=v_wide[b, t][:, j, :], in_=srcv, func=COPY, scale=gain)
 
-        def plane_engine(b, t, eh, j):
-            return "s" if j < PACK - PLANES[pieces.index((b, t, eh))] else "v"
+        def quad_tile(b, t, eh):
+            v_quad[b, t, eh] = work.tile([P, HALF, PACK], BF16, name="v_quad", align_bytes=64, bufs=DEPTH["v_quad"])
+            vq[b, t, eh] = keep.tile([P, HALF], U32, name=f"vq{b}{t}{eh}", align_bytes=64)
+            vq_s[b, t, eh] = keep.tile([P, HALF], U8, name=f"vqs{b}{t}{eh}", align_bytes=64)
 
-        def v_lay(b, t, eh):
-            by = MODES[pieces.index((b, t, eh))]
-            if by == "ps" or by == "pv":
-                for half in range(2):
-                    v_exit(b, t, eh, half, by[1])
-            else:
-                parts = 4 if by != "v" else 1
-                for part in range(parts):
-                    v_interleave(b, t, eh, by, part, parts)
-
-        def v_interleave(b, t, eh, engine, part, parts):
-            if not first(("vi", b, t, eh, part)):
-                return
-            for j in range(PACK):
-                v_widen(b, t, eh, j, plane_engine(b, t, eh, j))
-            if part > 0:
-                v_interleave(b, t, eh, engine, part - 1, parts)
-            if part == 0:
-                v_quad[b, t, eh] = work.tile([P, HALF, PACK], BF16, name="v_quad", align_bytes=64, bufs=3)
-            cols = slice(part * HALF // parts, (part + 1) * HALF // parts)
-            dst = v_quad[b, t, eh][:, cols, :].rearrange("p (c i) t -> p c t i", i=4)
-            srcv = v_wide[b, t, eh][:, :, cols].rearrange("p t (c i) -> p c t i", i=4)
+        def v_interleave(b, t, eh, engine, lo, hi):
+            dst = v_quad[b, t, eh][:, lo:hi, :].rearrange("p (c i) t -> p c t i", i=4)
+            srcv = v_wide[b, t][:, :, eh * HALF + lo:eh * HALF + hi].rearrange("p t (c i) -> p c t i", i=4)
             if engine == "v":
                 nc.vector.tensor_copy(out=dst, in_=srcv)
             elif engine == "g":
@@ -240,63 +278,48 @@ def tile_tensorsketchkeyvaluestate_w8_kernel(
             else:
                 nc.scalar.copy(out=dst, in_=srcv)
 
-        def v_turn(b, t, eh, half):
-            if not first(("vt", b, t, eh, half)):
-                return
-            for j in range(PACK):
-                v_widen(b, t, eh, j, plane_engine(b, t, eh, j))
-            bank = psum.tile([P, HALF // 2, PACK], BF16, name="bank_o", bufs=4)
-            for x in range(2):
-                cols = slice(half * HALF // 2 + x * P, half * HALF // 2 + (x + 1) * P)
-                nc.tensor.matmul(
-                    out=bank[:, x * P:(x + 1) * P, :],
-                    lhsT=ident_bf[:],
-                    rhs=v_wide[b, t, eh][:, :, cols].rearrange("p t n -> p n t"),
-                    start=True,
-                    stop=True,
-                )
-            turned[b, t, eh, half] = bank
-
-        def v_exit(b, t, eh, half, engine):
-            if not first(("vx", b, t, eh, half)):
-                return
-            if half == 1:
-                v_exit(b, t, eh, 0, engine)
-            v_turn(b, t, eh, half)
-            if half == 0:
-                v_quad[b, t, eh] = work.tile([P, HALF, PACK], BF16, name="v_quad", align_bytes=64, bufs=3)
-            dst = v_quad[b, t, eh][:, half * HALF // 2:(half + 1) * HALF // 2, :]
-            if engine == "v":
-                nc.vector.tensor_copy(out=dst, in_=turned[b, t, eh, half][:])
-            else:
-                nc.scalar.copy(out=dst, in_=turned[b, t, eh, half][:])
-
         def v_quantize(b, t, eh):
-            if not first(("vq", b, t, eh)):
-                return
-            v_lay(b, t, eh)
-            vq[b, t, eh] = keep.tile([P, HALF], U32, name=f"vq{b}{t}{eh}", align_bytes=64)
-            vq_s[b, t, eh] = keep.tile([P, HALF], U8, name=f"vqs{b}{t}{eh}", align_bytes=64)
             nc.vector.quantize_mx(
                 out=vq[b, t, eh][:].bitcast(FP8X4),
                 scales=vq_s[b, t, eh][:],
                 in_=v_quad[b, t, eh][:].rearrange("p n t -> p (n t)"),
             )
 
+        def add_v(b, t):
+            piece = b * GROUPS + t
+            at, step = W_AT[piece], W_STEP[piece]
+            add(at, ("wide_tile", b, t), "tile", 0, (), lambda: wide_tile(b, t), takes="v_wide")
+            for j in range(PACK):
+                engine = "v" if j >= PACK - PLANES[piece] else "s"
+                add(at + j * step, ("w", b, t, j), engine, 490 if engine == "v" else 920,
+                    (("load", "v", b, t), ("load", "v_gain"), ("wide_tile", b, t)),
+                    lambda j=j, engine=engine: v_widen(b, t, j, engine))
+            for eh in range(2):
+                slot = at + PACK * step + eh * I_STEP
+                engine = MODES[piece * 2 + eh]
+                parts = 1 if engine == "v" else 4
+                width = HALF // parts
+                each = {"v": 1120, "s": 560, "g": 600}[engine]
+                add(slot, ("quad_tile", b, t, eh), "tile", 0, (("w", b, t, 0),), lambda eh=eh: quad_tile(b, t, eh), takes="v_quad")
+                for part in range(parts):
+                    add(slot, ("lay", b, t, eh, part), engine, each,
+                        tuple([("w", b, t, j) for j in range(PACK)]) + (("quad_tile", b, t, eh),),
+                        lambda eh=eh, engine=engine, part=part, width=width: v_interleave(
+                            b, t, eh, engine, part * width, part * width + width),
+                        frees=(("wide_tile", b, t),))
+                add(slot + 1, ("vq", b, t, eh), "v", 510, tuple([("lay", b, t, eh, part) for part in range(parts)]),
+                    lambda eh=eh: v_quantize(b, t, eh), frees=(("quad_tile", b, t, eh),))
+
         units = [(b, h, t) for b in range(B) for h in range(HALVES) for t in range(GROUPS)]
-        p1_bank = {}
         p1_sb = {}
-        p2_bank = {}
+        p2_sb = {}
         phi = {}
         pq = {}
         pq_s = {}
 
         def p1_matmul(i, j):
-            if not first(("p1", i, j)):
-                return
-            k_quantize(units[i][0], units[i][2], j // 2)
             b, h, t = units[i]
-            bank = psum.tile([P, HALF], F32, name="bank_p1", bufs=2)
+            bank = psum.tile([P, HALF], F32, name="bank_p1", bufs=DEPTH["p1"])
             nc.tensor.matmul_mx(
                 out=bank[:],
                 lhsT=kq[b, t][:, j * P:(j + 1) * P].bitcast(FP8X4),
@@ -306,29 +329,21 @@ def tile_tensorsketchkeyvaluestate_w8_kernel(
                 start=True,
                 stop=True,
             )
-            p1_bank[i, j] = bank
+            banks["p1", i, j] = bank
+
+        def p1_tile(i):
+            p1_sb[i] = work.tile([P, PACK, HALF], F32, name="p1_sb", bufs=DEPTH["p1_sb"])
 
         def p1_gain(i, j):
-            if not first(("p1g", i, j)):
-                return
-            if j > 0:
-                p1_gain(i, j - 1)
-            p1_matmul(i, j)
             b, h, t = units[i]
-            if j == 0:
-                p1_sb[i] = work.tile([P, PACK, HALF], F32, name="p1_sb", bufs=3)
             nc.scalar.activation(
-                out=p1_sb[i][:, j, :], in_=p1_bank[i, j][:], func=COPY,
+                out=p1_sb[i][:, j, :], in_=banks["p1", i, j][:], func=COPY,
                 scale=g_f32[:, b * GROUPS + t, j:j + 1],
             )
 
         def p2_matmul(i, q):
-            if not first(("p2", i, q)):
-                return
-            for half in range(2):
-                k_quantize(units[i][0], units[i][2], half)
             b, h, t = units[i]
-            bank = psum.tile([P, PACK, P], F32, name="bank_p2", bufs=2)
+            bank = psum.tile([P, PACK, P], F32, name="bank_p2", bufs=DEPTH["p2"])
             f0 = h * HALF + q * P
             for j in range(PACK):
                 nc.tensor.matmul_mx(
@@ -340,68 +355,70 @@ def tile_tensorsketchkeyvaluestate_w8_kernel(
                     start=True,
                     stop=True,
                 )
-            p2_bank[i, q] = bank
+            banks["p2", i, q] = bank
 
-        def phi_mult(i, q):
-            if not first(("phi", i, q)):
-                return
-            for j in range(PACK):
-                p1_gain(i, j)
-            p2_matmul(i, q)
-            if q == 0:
-                phi[i] = work.tile([P, HALF, PACK], BF16, name="phi", align_bytes=64, bufs=3)
-            cols = slice(q * P, (q + 1) * P)
-            nc.vector.tensor_tensor(
-                out=phi[i][:, cols, :].rearrange("p (c i) t -> p c t i", i=2),
-                in0=p2_bank[i, q][:].rearrange("p t (c i) -> p c t i", i=2),
-                in1=p1_sb[i][:, :, cols].rearrange("p t (c i) -> p c t i", i=2),
-                op=MULT,
-            )
+        def phi_tile(i):
+            phi[i] = work.tile([P, HALF, PACK], BF16, name="phi", align_bytes=64, bufs=DEPTH["phi"])
+            pq[i] = keep.tile([P, HALF], U32, name=f"pq{i}", align_bytes=64)
+            pq_s[i] = keep.tile([P, HALF], U8, name=f"pqs{i}", align_bytes=64)
 
-        def phi_mult_g(i, q):
-            if not first(("phi", i, q)):
-                return
-            for j in range(PACK):
-                p1_gain(i, j)
-            p2_matmul(i, q)
-            if q == 0:
-                phi[i] = work.tile([P, HALF, PACK], BF16, name="phi", align_bytes=64, bufs=3)
-            p2_sb = work.tile([P, PACK, P], F32, name="p2_sb", bufs=2)
-            nc.scalar.copy(out=p2_sb[:], in_=p2_bank[i, q][:])
+        def p2_copy(i, q):
+            p2_sb[i, q] = work.tile([P, PACK, P], F32, name="p2_sb", bufs=DEPTH["p2_sb"])
+            nc.scalar.copy(out=p2_sb[i, q][:], in_=banks["p2", i, q][:])
+
+        def multiply(i, q, engine):
             cols = slice(q * P, (q + 1) * P)
-            nc.gpsimd.tensor_tensor(
+            second = banks["p2", i, q] if engine == "v" else p2_sb[i, q]
+            (nc.vector if engine == "v" else nc.gpsimd).tensor_tensor(
                 out=phi[i][:, cols, :].rearrange("p (c i) t -> p c t i", i=4),
-                in0=p2_sb[:].rearrange("p t (c i) -> p c t i", i=4),
+                in0=second[:].rearrange("p t (c i) -> p c t i", i=4),
                 in1=p1_sb[i][:, :, cols].rearrange("p t (c i) -> p c t i", i=4),
                 op=MULT,
             )
 
         def phi_quantize(i):
-            if not first(("pq", i)):
-                return
-            pq[i] = keep.tile([P, HALF], U32, name=f"pq{i}", align_bytes=64)
-            pq_s[i] = keep.tile([P, HALF], U8, name=f"pqs{i}", align_bytes=64)
             nc.vector.quantize_mx(
                 out=pq[i][:].bitcast(FP8X4),
                 scales=pq_s[i][:],
                 in_=phi[i][:].rearrange("p n t -> p (n t)"),
             )
 
-        out_bank = {}
+        def add_unit(i):
+            b, h, t = units[i]
+            slot = QUARTERS * i
+            add(slot - LEAD, ("p1_tile", i), "tile", 0, (), lambda: p1_tile(i), takes="p1_sb")
+            add(slot, ("phi_tile", i), "tile", 0, (), lambda: phi_tile(i), takes="phi")
+            for j in range(PACK):
+                add(slot + j - LEAD, ("p1", i, j), "t", 230,
+                    (k_ready(b, t)[min(j // 2, len(k_ready(b, t)) - 1)], ("load", "u", h, 0), ("load", "us", 0)),
+                    lambda j=j: p1_matmul(i, j), takes="p1")
+                add(slot + j - LEAD, ("g1", i, j), "s", 530, (("p1", i, j), ("p1_tile", i), ("g_f32",)),
+                    lambda j=j: p1_gain(i, j), frees=(("p1", i, j),))
+            gains = tuple([("g1", i, j) for j in range(PACK)])
+            for q in range(QUARTERS):
+                add(slot + q - 2, ("p2", i, q), "t", 270, k_ready(b, t) + (("load", "u", h, 1), ("load", "us", 1)),
+                    lambda q=q: p2_matmul(i, q), takes="p2")
+                if GMASK[i] >> q & 1:
+                    add(slot + q - 1, ("p2c", i, q), "s", 500, (("p2", i, q),), lambda q=q: p2_copy(i, q), takes="p2_sb", frees=(("p2", i, q),))
+                    add(slot + q, ("mul", i, q), "g", 920, (("p2c", i, q), ("phi_tile", i)) + gains,
+                        lambda q=q: multiply(i, q, "g"), frees=(("p2c", i, q), ("p1_tile", i)))
+                else:
+                    add(slot + q, ("mul", i, q), "v", 490, (("p2", i, q), ("phi_tile", i)) + gains,
+                        lambda q=q: multiply(i, q, "v"), frees=(("p2", i, q), ("p1_tile", i)))
+            add(slot + QUARTERS + 1, ("pq", i), "v", 510, tuple([("mul", i, q) for q in range(QUARTERS)]),
+                lambda: phi_quantize(i), frees=(("phi_tile", i),))
+
+        out_sb = {}
 
         def place(n):
             b, rest = divmod(n, OUT_BANKS // B)
-            outer, ft = divmod(rest, QUARTERS)
-            h, eh = divmod(outer, 2) if b < B - 1 else (outer % 2, outer // 2)
-            return b, h * QUARTERS + ft, eh
+            c, eh = divmod(rest, 2)
+            return b, c, eh
 
         def out_matmul(n):
             b, c, eh = place(n)
             h, ft = divmod(c, QUARTERS)
-            for t in range(GROUPS):
-                phi_quantize((b * HALVES + h) * GROUPS + t)
-                v_quantize(b, t, eh)
-            bank = psum.tile([P, HALF], F32, name="bank_o", bufs=4)
+            bank = psum.tile([P, HALF], F32, name="bank_o", bufs=DEPTH["o"])
             for t in range(GROUPS):
                 i = (b * HALVES + h) * GROUPS + t
                 nc.tensor.matmul_mx(
@@ -413,77 +430,58 @@ def tile_tensorsketchkeyvaluestate_w8_kernel(
                     start=(t == 0),
                     stop=(t == GROUPS - 1),
                 )
-            out_bank[n] = bank
+            banks["out", n] = bank
+
+        def out_tile(n):
+            b, c, eh = place(n)
+            out_sb[b, c] = work.tile([P, E], F32, name="out_sb", bufs=DEPTH["out_sb"])
 
         def out_sum(n):
             b, c, eh = place(n)
-            total = work.tile([P, HALF], F32, name="out_sb", bufs=6)
             cols = slice(eh * HALF, (eh + 1) * HALF)
             nc.vector.scalar_tensor_tensor(
-                out=total[:], in0=s0_rows[b][:, c, cols], scalar=a_f32[:, c:c + 1],
-                in1=out_bank[n][:], op0=MULT, op1=ADD,
+                out=out_sb[b, c][:, cols], in0=s0_rows[b][:, c, cols], scalar=a_f32[:, c:c + 1],
+                in1=banks["out", n][:], op0=MULT, op1=ADD,
             )
-            nc.sync.dma_start(out=out[b, c * P:(c + 1) * P, cols], in_=total[:])
 
-        def a_columns():
-            nc.scalar.copy(out=a_pad[0:F // P, :], in_=a_bf[:])
-            bank = psum.tile([P, P], F32, name="bank_o", bufs=4)
-            nc.tensor.transpose(bank[:], a_pad[:], ident[:])
-            nc.scalar.copy(out=a_f32[:], in_=bank[:, 0:F // P])
+        def out_store(n, both):
+            b, c, eh = place(n)
+            cols = slice(0, E) if both else slice(eh * HALF, (eh + 1) * HALF)
+            nc.sync.dma_start(out=out[b, c * P:(c + 1) * P, cols], in_=out_sb[b, c][:, cols])
 
-        k_transpose(0, 0, 0)
-        k_transpose(0, 0, 1)
-        k_copy(0, 0, 0, "v")
-        nc.vector.tensor_copy(out=g_f32[:], in_=g_bf[:])
-        k_copy(0, 0, 1, "s")
-        k_quantize(0, 0, 0)
-        k_quantize(0, 0, 1)
-        for j in range(PACK):
-            p1_gain(0, j)
-        p2_matmul(0, 0)
-        p2_matmul(0, 1)
-        k_transpose(0, 1, 0)
-        k_transpose(0, 1, 1)
-        v_lay(*pieces[0])
-        k_quantize(0, 1, 0)
-        k_quantize(0, 1, 1)
+        def add_out(n, slot):
+            b, c, eh = place(n)
+            i = (b * HALVES + c // QUARTERS) * GROUPS
+            if eh == 0:
+                add(slot, ("out_tile", n), "tile", 0, (), lambda: out_tile(n), takes="out_sb")
+            add(slot - 2, ("out", n), "t", 450, (("pq", i), ("pq", i + 1), ("vq", b, 0, eh), ("vq", b, 1, eh)),
+                lambda: out_matmul(n), takes="o")
+            add(slot, ("sum", n), "v", 490, (("out", n), ("out_tile", n - eh), ("load", "s0", b, c // QUARTERS), ("a_f32",)),
+                lambda: out_sum(n), frees=(("out", n),))
+            if n >= OUT_BANKS - 2:
+                add(slot, ("store", n), "store", 450, (("sum", n),), lambda: out_store(n, False), frees=(("out_tile", n - eh),))
+            elif eh == 1:
+                add(slot, ("store", n), "store", 900, (("sum", n), ("sum", n - 1)), lambda: out_store(n, True), frees=(("out_tile", n - 1),))
 
-        for s in range(SLOTS + OUT_BANKS):
-            i, q = divmod(s, QUARTERS)
-            if s < SLOTS:
-                (phi_mult_g if GM_FIRST <= i < GM_LAST and q in GM_Q else phi_mult)(i, q)
-            if q == 1 and 0 < i <= UNITS:
-                phi_quantize(i - 1)
-            if s == 1:
-                v_quantize(*pieces[0])
-                a_columns()
-            if s + 2 < SLOTS:
-                p2_matmul((s + 2) // QUARTERS, (s + 2) % QUARTERS)
-            for x in range(QUARTERS, min(s + LEAD + 1, SLOTS)):
-                p1_gain(x // QUARTERS, x % QUARTERS)
-            for t, at in ((0, KA), (1, KB)):
-                if s == at:
-                    k_transpose(1, t, 0)
-                    k_transpose(1, t, 1)
-                if s == at + 1:
-                    k_copy(1, t, 0, "s")
-                    k_copy(1, t, 1, "s")
-                if s == at + 2:
-                    k_quantize(1, t, 0)
-                    k_quantize(1, t, 1)
-            for m in range(1, 8):
-                at, step = (VA + VSTEP * (m - 1), VSTEP) if m < 4 else (VB + VSTEPB * (m - 4), VSTEPB)
-                b, t, eh = pieces[m]
-                for j in range(PACK):
-                    if s == at + j * step // PACK:
-                        v_widen(b, t, eh, j, plane_engine(b, t, eh, j))
-                if s == at + step:
-                    v_lay(b, t, eh)
-                if s == at + step + 1:
-                    v_quantize(b, t, eh)
-            for o in range(8):
-                for x in range(QUARTERS):
-                    if s == OUT_AT[o] + x - 2:
-                        out_matmul(o * QUARTERS + x)
-                    if s == OUT_AT[o] + x:
-                        out_sum(o * QUARTERS + x)
+        def a_transpose():
+            banks["a"] = psum.tile([P, P], F32, name="bank_o", bufs=DEPTH["o"])
+            nc.tensor.transpose(banks["a"][:], a_pad[:], ident[:])
+
+        add(1, ("a_row",), "s", 200, (("load", "a"),), lambda: nc.scalar.copy(out=a_pad[0:F // P, :], in_=a_bf[:]))
+        add(1, ("a_turn",), "t", 105, (("a_row",),), a_transpose, takes="o")
+        add(1, ("a_f32",), "s", 80, (("a_turn",),), lambda: nc.scalar.copy(out=a_f32[:], in_=banks["a"][:, 0:F // P]), frees=(("a_turn",),))
+
+        add_k(-90, 0, 0)
+        add_k(-1, 0, 1)
+        add_k(KA, 1, 0)
+        add_k(KB, 1, 1)
+        for i in range(UNITS):
+            add_unit(i)
+        for b in range(B):
+            for t in range(GROUPS):
+                add_v(b, t)
+        for n in range(OUT_BANKS):
+            add_out(n, OUT_AT[n // 4] + n % 4)
+
+        tasks.sort(key=lambda x: (x[0], x[1]))
+        issue_in_start_order([x[2] for x in tasks])

from contextlib import ExitStack

import concourse.mybir as mybir
from concourse.masks import make_identity

B, T, D, F, E = 2, 1024, 512, 1024, 1024

FLOPS = 2 * B * T * D * F * 2 + 2 * B * T * F * E

F32 = mybir.dt.float32
BF16 = mybir.dt.bfloat16
U32 = mybir.dt.uint32
I32 = mybir.dt.int32
U8 = mybir.dt.uint8
FP8 = mybir.dt.float8_e4m3fn
FP8X4 = mybir.dt.float8_e4m3fn_x4

COPY = mybir.ActivationFunctionType.Copy
MULT = mybir.AluOpType.mult
ADD = mybir.AluOpType.add

P = 128
PACK = 4
GROUP = P * PACK
GROUPS = T // GROUP
HALF = 512
HALVES = F // HALF
QUARTERS = HALF // P
UNITS = B * HALVES * GROUPS
SLOTS = UNITS * QUARTERS
OUT_BANKS = B * (F // P) * (E // HALF)

LEAD = 6
W_AT = (8, 0, 8, 14)
W_STEP = (3, 2, 2, 2)
I_STEP = 2
KA = 6
KB = 10
OUT_AT = (14, 19, 21, 27, 40, 41, 45, 55)
MODES = ("v", "v", "v", "g", "g", "g", "g", "s")
PLANES = (3, 1, 0, 0)
GMASK = (0, 4, 0, 0, 8, 8, 8, 10)
LAG = 90
PORT = 1

DEPTH = {"p1": 2, "p2": 2, "o": 4, "p1_sb": 3, "p2_sb": 2, "phi": 3, "k_quad": 2, "v_wide": 2, "v_quad": 3, "out_sb": 4}


def issue_in_start_order(tasks):
    free, finish, freed, readers, tenants = {}, {}, {}, {}, {}
    for name, engine, weight, needs, takes, frees, issue in tasks:
        for tile in frees:
            readers[tile] = readers.get(tile, 0) + 1
    waiting = list(tasks)
    while waiting:
        best = None
        for task in waiting:
            name, engine, weight, needs, takes, frees, issue = task
            if not all([n in finish for n in needs]):
                continue
            port = engine == "g" or engine == "v" and name[0] in ("kq", "vq", "pq", "w", "lay")
            start = max([free.get(engine, 0)] + [finish[n] for n in needs])
            if port and PORT:
                start = max(start, free.get("port", 0))
            if takes is not None:
                held = tenants.setdefault(takes, [])
                if len(held) >= DEPTH[takes]:
                    old = held[len(held) - DEPTH[takes]]
                    if readers.get(old, 0) > 0:
                        continue
                    start = max(start, freed[old])
            if best is None or start < best[0]:
                best = (start, task)
        start, task = best
        name, engine, weight, needs, takes, frees, issue = task
        waiting.remove(task)
        issue()
        free[engine] = start + weight
        if engine == "g" or engine == "v" and name[0] in ("kq", "vq", "pq", "w", "lay"):
            free["port"] = start + weight
        lag = {"load": 1900, "store": 2000, "tile": 0}.get(engine, LAG)
        finish[name] = start + weight + lag
        if takes is not None:
            tenants[takes].append(name)
        for tile in frees:
            readers[tile] = readers[tile] - 1
            freed[tile] = max(freed.get(tile, 0), finish[name])


def tile_tensorsketchkeyvaluestate_w8_kernel(
    tc, k, u1_words, u1_scales, u2_words, u2_scales, g, v_bytes, v_scale, a, s0, out
):
    nc = tc.nc
    with ExitStack() as ctx:
        keep = ctx.enter_context(tc.tile_pool(name="keep", bufs=1))
        work = ctx.enter_context(tc.tile_pool(name="work", bufs=2))
        psum = ctx.enter_context(tc.psum_pool(name="psum", bufs=2))
        ctx.enter_context(tc.manual_schedule())

        tasks = []

        def add(slot, name, engine, weight, needs, issue, takes=None, frees=()):
            tasks.append((slot, len(tasks), (name, engine, weight, needs, takes, frees, issue)))

        u_scale = []
        for w in range(2):
            plane = keep.tile([P, F], U8, name=f"u_scale{w}", align_bytes=64)
            nc.vector.memset(plane[:].bitcast(I32), 0)
            u_scale.append(plane)
        ident = keep.tile([P, P], F32, name="ident")
        make_identity(nc, ident[:])
        warm = keep.tile([P, 1], F32, name="warm")
        nc.vector.memset(warm[:], 0.0)
        warm_out = keep.tile([P, 1], F32, name="warm_out")
        a_pad = keep.tile([P, P], F32, name="a_pad")
        nc.vector.memset(a_pad[:], 0.0)

        k_rows = {}
        v_code = {}
        for b in range(B):
            for t in range(GROUPS):
                k_rows[b, t] = keep.tile([P, PACK, D], BF16, name=f"k_rows{b}{t}", align_bytes=64)
                v_code[b, t] = keep.tile([P, PACK, E], U8, name=f"v_code{b}{t}", align_bytes=64)
        u_code = keep.tile([P, 2, F], U32, name="u_code", align_bytes=64)
        s0_rows = [keep.tile([P, F // P, E], BF16, name=f"s0_rows{b}", align_bytes=64) for b in range(B)]
        v_gain = keep.tile([P, GROUPS, PACK], F32, name="v_gain")
        g_bf = keep.tile([P, B * GROUPS, PACK], BF16, name="g_bf")
        a_bf = keep.tile([F // P, P], BF16, name="a_bf")
        g_f32 = keep.tile([P, B * GROUPS, PACK], F32, name="g_f32")
        a_f32 = keep.tile([P, F // P], F32, name="a_f32")

        def load_k(b, t, lo, hi):
            rows = k[b].rearrange("(t p j) d -> t p j d", p=P, j=PACK)[t]
            nc.sync.dma_start(out=k_rows[b, t][:, lo:hi, :], in_=rows[:, lo:hi, :])

        def load_v(b, t):
            rows = v_bytes[b].rearrange("(t p j) e -> t p j e", p=P, j=PACK)[t]
            nc.sync.dma_start(out=v_code[b, t][:], in_=rows)

        def load_u(h, w):
            words = (u1_words, u2_words)[w].rearrange("o p n t -> p (o n t)")
            cols = slice(h * HALF * PACK, (h + 1) * HALF * PACK)
            nc.sync.dma_start(out=u_code[:, w, h * HALF:(h + 1) * HALF].bitcast(I32), in_=words[:, cols].bitcast(I32))

        def load_us(w):
            scales = (u1_scales, u2_scales)[w]
            for q in range(4):
                nc.sync.dma_start(
                    out=u_scale[w][32 * q:32 * q + 4, :].bitcast(I32),
                    in_=scales[0, 4 * q:4 * q + 4, :].bitcast(I32),
                )

        def load_s0(b, half):
            rows = s0[b].rearrange("(c p) e -> p c e", p=P)
            chunk = slice(half * QUARTERS, (half + 1) * QUARTERS)
            nc.sync.dma_start(out=s0_rows[b][:, chunk, :], in_=rows[:, chunk, :])

        def load_v_gain():
            nc.scalar.dma_start(out=v_gain[:], in_=v_scale.rearrange("o (t p j) x -> p (o t) (j x)", p=P, j=PACK))

        def load_g():
            nc.scalar.dma_start(out=g_bf[:], in_=g.rearrange("b (t p j) -> p (b t) j", p=P, j=PACK))

        def load_a():
            nc.scalar.dma_start(out=a_bf[:], in_=a.rearrange("(c p) -> c p", p=P))

        def load(name, weight, issue):
            add(-100, ("load",) + name, "load", weight, (), issue)

        load(("v_gain",), 30, load_v_gain)
        load(("k", 0, 0, 0), 440, lambda: load_k(0, 0, 0, 2))
        load(("us", 0), 300, lambda: load_us(0))
        load(("k", 0, 0, 1), 440, lambda: load_k(0, 0, 2, 4))
        load(("v", 0, 0), 870, lambda: load_v(0, 0))
        load(("u", 0, 0), 440, lambda: load_u(0, 0))
        load(("us", 1), 300, lambda: load_us(1))
        load(("g",), 30, load_g)
        load(("u", 0, 1), 440, lambda: load_u(0, 1))
        load(("k", 0, 1), 870, lambda: load_k(0, 1, 0, 4))
        load(("v", 0, 1), 870, lambda: load_v(0, 1))
        load(("u", 1, 0), 440, lambda: load_u(1, 0))
        load(("u", 1, 1), 440, lambda: load_u(1, 1))
        load(("a",), 30, load_a)
        load(("k", 1, 0), 870, lambda: load_k(1, 0, 0, 4))
        load(("s0", 0, 0), 1750, lambda: load_s0(0, 0))
        load(("v", 1, 0), 870, lambda: load_v(1, 0))
        load(("k", 1, 1), 870, lambda: load_k(1, 1, 0, 4))
        load(("v", 1, 1), 870, lambda: load_v(1, 1))
        load(("s0", 0, 1), 1750, lambda: load_s0(0, 1))
        load(("s0", 1, 0), 1750, lambda: load_s0(1, 0))
        load(("s0", 1, 1), 1750, lambda: load_s0(1, 1))

        nc.scalar.activation(out=warm_out[:], in_=warm[:], func=COPY, scale=warm[:])
        add(-1, ("g_f32",), "v", 70, (("load", "g"),), lambda: nc.vector.tensor_copy(out=g_f32[:], in_=g_bf[:]))

        banks = {}
        k_quad = {}
        kq = {}
        kq_s = {}

        def k_transpose(b, t, half):
            bank = psum.tile([P, 2, 2, P], F32, name="bank_o", bufs=DEPTH["o"])
            words = k_rows[b, t][:].rearrange("p j d -> p (j d)").bitcast(F32)
            for jj in range(2):
                j0 = (2 * half + jj) * (D // 2)
                for u in range(2):
                    nc.tensor.transpose(bank[:, jj, u, :], words[:, j0 + u:j0 + D // 2:2], ident[:])
            banks["kt", b, t, half] = bank

        def k_tiles(b, t):
            k_quad[b, t] = work.tile([P, GROUP * PACK], BF16, name="k_quad", align_bytes=64, bufs=DEPTH["k_quad"])
            kq[b, t] = keep.tile([P, GROUP], U32, name=f"kq{b}{t}", align_bytes=64)
            kq_s[b, t] = keep.tile([P, GROUP], U8, name=f"kqs{b}{t}", align_bytes=64)

        def k_copy(b, t, half, engine):
            width = GROUP * PACK // 2
            dst = k_quad[b, t][:, half * width:(half + 1) * width].bitcast(F32)
            dst = dst.rearrange("p (j m u) -> p j m u", j=2, u=2)
            srcv = banks["kt", b, t, half][:].rearrange("p j u m -> p j m u")
            if engine == "v":
                nc.vector.tensor_copy(out=dst, in_=srcv)
            else:
                nc.scalar.copy(out=dst, in_=srcv)

        def k_quantize(b, t, lo, hi):
            nc.vector.quantize_mx(
                out=kq[b, t][:, lo:hi].bitcast(FP8X4),
                scales=kq_s[b, t][:, lo:hi],
                in_=k_quad[b, t][:, lo * PACK:hi * PACK],
            )

        def add_k(slot, b, t):
            add(slot, ("k_tiles", b, t), "tile", 0, (), lambda: k_tiles(b, t), takes="k_quad")
            for half in range(2):
                source = ("load", "k", b, t) + ((half,) if (b, t) == (0, 0) else ())
                engine = "v" if (b, t, half) == (0, 0, 0) else "s"
                add(slot, ("kt", b, t, half), "t", 420, (source,), lambda half=half: k_transpose(b, t, half), takes="o")
                add(slot, ("kc", b, t, half), engine, 490, (("kt", b, t, half), ("k_tiles", b, t)),
                    lambda half=half, engine=engine: k_copy(b, t, half, engine), frees=(("kt", b, t, half),))
                if (b, t) == (0, 0):
                    add(slot, ("kq", b, t, half), "v", 290, (("kc", b, t, half),),
                        lambda half=half: k_quantize(b, t, half * 256, half * 256 + 256), frees=(("k_tiles", b, t),))
            if (b, t) != (0, 0):
                add(slot, ("kq", b, t, 0), "v", 510, (("kc", b, t, 0), ("kc", b, t, 1)),
                    lambda: k_quantize(b, t, 0, GROUP), frees=(("k_tiles", b, t),))

        def k_ready(b, t):
            return (("kq", b, t, 0), ("kq", b, t, 1)) if (b, t) == (0, 0) else (("kq", b, t, 0),)

        v_wide = {}
        v_quad = {}
        vq = {}
        vq_s = {}

        def wide_tile(b, t):
            v_wide[b, t] = work.tile([P, PACK, E], BF16, name="v_wide", align_bytes=64, bufs=DEPTH["v_wide"])

        def v_widen(b, t, j, engine):
            srcv = v_code[b, t][:, j, :].bitcast(FP8)
            gain = v_gain[:, t, j:j + 1]
            if engine == "v":
                nc.vector.tensor_scalar(out=v_wide[b, t][:, j, :], in0=srcv, scalar1=gain, scalar2=None, op0=MULT)
            else:
                nc.scalar.activation(out=v_wide[b, t][:, j, :], in_=srcv, func=COPY, scale=gain)

        def quad_tile(b, t, eh):
            v_quad[b, t, eh] = work.tile([P, HALF, PACK], BF16, name="v_quad", align_bytes=64, bufs=DEPTH["v_quad"])
            vq[b, t, eh] = keep.tile([P, HALF], U32, name=f"vq{b}{t}{eh}", align_bytes=64)
            vq_s[b, t, eh] = keep.tile([P, HALF], U8, name=f"vqs{b}{t}{eh}", align_bytes=64)

        def v_interleave(b, t, eh, engine, lo, hi):
            dst = v_quad[b, t, eh][:, lo:hi, :].rearrange("p (c i) t -> p c t i", i=4)
            srcv = v_wide[b, t][:, :, eh * HALF + lo:eh * HALF + hi].rearrange("p t (c i) -> p c t i", i=4)
            if engine == "v":
                nc.vector.tensor_copy(out=dst, in_=srcv)
            elif engine == "g":
                nc.gpsimd.tensor_scalar(out=dst, in0=srcv, scalar1=1.0, scalar2=0.0, op0=MULT, op1=ADD)
            else:
                nc.scalar.copy(out=dst, in_=srcv)

        def v_quantize(b, t, eh):
            nc.vector.quantize_mx(
                out=vq[b, t, eh][:].bitcast(FP8X4),
                scales=vq_s[b, t, eh][:],
                in_=v_quad[b, t, eh][:].rearrange("p n t -> p (n t)"),
            )

        def add_v(b, t):
            piece = b * GROUPS + t
            at, step = W_AT[piece], W_STEP[piece]
            add(at, ("wide_tile", b, t), "tile", 0, (), lambda: wide_tile(b, t), takes="v_wide")
            for j in range(PACK):
                engine = "v" if j >= PACK - PLANES[piece] else "s"
                add(at + j * step, ("w", b, t, j), engine, 490 if engine == "v" else 920,
                    (("load", "v", b, t), ("load", "v_gain"), ("wide_tile", b, t)),
                    lambda j=j, engine=engine: v_widen(b, t, j, engine))
            for eh in range(2):
                slot = at + PACK * step + eh * I_STEP
                engine = MODES[piece * 2 + eh]
                parts = 1 if engine == "v" else 4
                width = HALF // parts
                each = {"v": 1120, "s": 560, "g": 600}[engine]
                add(slot, ("quad_tile", b, t, eh), "tile", 0, (("w", b, t, 0),), lambda eh=eh: quad_tile(b, t, eh), takes="v_quad")
                for part in range(parts):
                    add(slot, ("lay", b, t, eh, part), engine, each,
                        tuple([("w", b, t, j) for j in range(PACK)]) + (("quad_tile", b, t, eh),),
                        lambda eh=eh, engine=engine, part=part, width=width: v_interleave(
                            b, t, eh, engine, part * width, part * width + width),
                        frees=(("wide_tile", b, t),))
                add(slot + 1, ("vq", b, t, eh), "v", 510, tuple([("lay", b, t, eh, part) for part in range(parts)]),
                    lambda eh=eh: v_quantize(b, t, eh), frees=(("quad_tile", b, t, eh),))

        units = [(b, h, t) for b in range(B) for h in range(HALVES) for t in range(GROUPS)]
        p1_sb = {}
        p2_sb = {}
        phi = {}
        pq = {}
        pq_s = {}

        def p1_matmul(i, j):
            b, h, t = units[i]
            bank = psum.tile([P, HALF], F32, name="bank_p1", bufs=DEPTH["p1"])
            nc.tensor.matmul_mx(
                out=bank[:],
                lhsT=kq[b, t][:, j * P:(j + 1) * P].bitcast(FP8X4),
                lhsT_scale=kq_s[b, t][:, j * P:(j + 1) * P],
                rhs=u_code[:, 0, h * HALF:(h + 1) * HALF].bitcast(FP8X4),
                rhs_scale=u_scale[0][:, h * HALF:(h + 1) * HALF],
                start=True,
                stop=True,
            )
            banks["p1", i, j] = bank

        def p1_tile(i):
            p1_sb[i] = work.tile([P, PACK, HALF], F32, name="p1_sb", bufs=DEPTH["p1_sb"])

        def p1_gain(i, j):
            b, h, t = units[i]
            nc.scalar.activation(
                out=p1_sb[i][:, j, :], in_=banks["p1", i, j][:], func=COPY,
                scale=g_f32[:, b * GROUPS + t, j:j + 1],
            )

        def p2_matmul(i, q):
            b, h, t = units[i]
            bank = psum.tile([P, PACK, P], F32, name="bank_p2", bufs=DEPTH["p2"])
            f0 = h * HALF + q * P
            for j in range(PACK):
                nc.tensor.matmul_mx(
                    out=bank[:, j, :],
                    lhsT=kq[b, t][:, j * P:(j + 1) * P].bitcast(FP8X4),
                    lhsT_scale=kq_s[b, t][:, j * P:(j + 1) * P],
                    rhs=u_code[:, 1, f0:f0 + P].bitcast(FP8X4),
                    rhs_scale=u_scale[1][:, f0:f0 + P],
                    start=True,
                    stop=True,
                )
            banks["p2", i, q] = bank

        def phi_tile(i):
            phi[i] = work.tile([P, HALF, PACK], BF16, name="phi", align_bytes=64, bufs=DEPTH["phi"])
            pq[i] = keep.tile([P, HALF], U32, name=f"pq{i}", align_bytes=64)
            pq_s[i] = keep.tile([P, HALF], U8, name=f"pqs{i}", align_bytes=64)

        def p2_copy(i, q):
            p2_sb[i, q] = work.tile([P, PACK, P], F32, name="p2_sb", bufs=DEPTH["p2_sb"])
            nc.scalar.copy(out=p2_sb[i, q][:], in_=banks["p2", i, q][:])

        def multiply(i, q, engine):
            cols = slice(q * P, (q + 1) * P)
            second = banks["p2", i, q] if engine == "v" else p2_sb[i, q]
            (nc.vector if engine == "v" else nc.gpsimd).tensor_tensor(
                out=phi[i][:, cols, :].rearrange("p (c i) t -> p c t i", i=4),
                in0=second[:].rearrange("p t (c i) -> p c t i", i=4),
                in1=p1_sb[i][:, :, cols].rearrange("p t (c i) -> p c t i", i=4),
                op=MULT,
            )

        def phi_quantize(i):
            nc.vector.quantize_mx(
                out=pq[i][:].bitcast(FP8X4),
                scales=pq_s[i][:],
                in_=phi[i][:].rearrange("p n t -> p (n t)"),
            )

        def add_unit(i):
            b, h, t = units[i]
            slot = QUARTERS * i
            add(slot - LEAD, ("p1_tile", i), "tile", 0, (), lambda: p1_tile(i), takes="p1_sb")
            add(slot, ("phi_tile", i), "tile", 0, (), lambda: phi_tile(i), takes="phi")
            for j in range(PACK):
                add(slot + j - LEAD, ("p1", i, j), "t", 230,
                    (k_ready(b, t)[min(j // 2, len(k_ready(b, t)) - 1)], ("load", "u", h, 0), ("load", "us", 0)),
                    lambda j=j: p1_matmul(i, j), takes="p1")
                add(slot + j - LEAD, ("g1", i, j), "s", 530, (("p1", i, j), ("p1_tile", i), ("g_f32",)),
                    lambda j=j: p1_gain(i, j), frees=(("p1", i, j),))
            gains = tuple([("g1", i, j) for j in range(PACK)])
            for q in range(QUARTERS):
                add(slot + q - 2, ("p2", i, q), "t", 270, k_ready(b, t) + (("load", "u", h, 1), ("load", "us", 1)),
                    lambda q=q: p2_matmul(i, q), takes="p2")
                if GMASK[i] >> q & 1:
                    add(slot + q - 1, ("p2c", i, q), "s", 500, (("p2", i, q),), lambda q=q: p2_copy(i, q), takes="p2_sb", frees=(("p2", i, q),))
                    add(slot + q, ("mul", i, q), "g", 920, (("p2c", i, q), ("phi_tile", i)) + gains,
                        lambda q=q: multiply(i, q, "g"), frees=(("p2c", i, q), ("p1_tile", i)))
                else:
                    add(slot + q, ("mul", i, q), "v", 490, (("p2", i, q), ("phi_tile", i)) + gains,
                        lambda q=q: multiply(i, q, "v"), frees=(("p2", i, q), ("p1_tile", i)))
            add(slot + QUARTERS + 1, ("pq", i), "v", 510, tuple([("mul", i, q) for q in range(QUARTERS)]),
                lambda: phi_quantize(i), frees=(("phi_tile", i),))

        out_sb = {}

        def place(n):
            b, rest = divmod(n, OUT_BANKS // B)
            c, eh = divmod(rest, 2)
            return b, c, eh

        def out_matmul(n):
            b, c, eh = place(n)
            h, ft = divmod(c, QUARTERS)
            bank = psum.tile([P, HALF], F32, name="bank_o", bufs=DEPTH["o"])
            for t in range(GROUPS):
                i = (b * HALVES + h) * GROUPS + t
                nc.tensor.matmul_mx(
                    out=bank[:],
                    lhsT=pq[i][:, ft * P:(ft + 1) * P].bitcast(FP8X4),
                    lhsT_scale=pq_s[i][:, ft * P:(ft + 1) * P],
                    rhs=vq[b, t, eh][:].bitcast(FP8X4),
                    rhs_scale=vq_s[b, t, eh][:],
                    start=(t == 0),
                    stop=(t == GROUPS - 1),
                )
            banks["out", n] = bank

        def out_tile(n):
            b, c, eh = place(n)
            out_sb[b, c] = work.tile([P, E], F32, name="out_sb", bufs=DEPTH["out_sb"])

        def out_sum(n):
            b, c, eh = place(n)
            cols = slice(eh * HALF, (eh + 1) * HALF)
            nc.vector.scalar_tensor_tensor(
                out=out_sb[b, c][:, cols], in0=s0_rows[b][:, c, cols], scalar=a_f32[:, c:c + 1],
                in1=banks["out", n][:], op0=MULT, op1=ADD,
            )

        def out_store(n, both):
            b, c, eh = place(n)
            cols = slice(0, E) if both else slice(eh * HALF, (eh + 1) * HALF)
            nc.sync.dma_start(out=out[b, c * P:(c + 1) * P, cols], in_=out_sb[b, c][:, cols])

        def add_out(n, slot):
            b, c, eh = place(n)
            i = (b * HALVES + c // QUARTERS) * GROUPS
            if eh == 0:
                add(slot, ("out_tile", n), "tile", 0, (), lambda: out_tile(n), takes="out_sb")
            add(slot - 2, ("out", n), "t", 450, (("pq", i), ("pq", i + 1), ("vq", b, 0, eh), ("vq", b, 1, eh)),
                lambda: out_matmul(n), takes="o")
            add(slot, ("sum", n), "v", 490, (("out", n), ("out_tile", n - eh), ("load", "s0", b, c // QUARTERS), ("a_f32",)),
                lambda: out_sum(n), frees=(("out", n),))
            if n >= OUT_BANKS - 2:
                add(slot, ("store", n), "store", 450, (("sum", n),), lambda: out_store(n, False), frees=(("out_tile", n - eh),))
            elif eh == 1:
                add(slot, ("store", n), "store", 900, (("sum", n), ("sum", n - 1)), lambda: out_store(n, True), frees=(("out_tile", n - 1),))

        def a_transpose():
            banks["a"] = psum.tile([P, P], F32, name="bank_o", bufs=DEPTH["o"])
            nc.tensor.transpose(banks["a"][:], a_pad[:], ident[:])

        add(1, ("a_row",), "s", 200, (("load", "a"),), lambda: nc.scalar.copy(out=a_pad[0:F // P, :], in_=a_bf[:]))
        add(1, ("a_turn",), "t", 105, (("a_row",),), a_transpose, takes="o")
        add(1, ("a_f32",), "s", 80, (("a_turn",),), lambda: nc.scalar.copy(out=a_f32[:], in_=banks["a"][:, 0:F // P]), frees=(("a_turn",),))

        add_k(-90, 0, 0)
        add_k(-1, 0, 1)
        add_k(KA, 1, 0)
        add_k(KB, 1, 1)
        for i in range(UNITS):
            add_unit(i)
        for b in range(B):
            for t in range(GROUPS):
                add_v(b, t)
        for n in range(OUT_BANKS):
            add_out(n, OUT_AT[n // 4] + n % 4)

        tasks.sort(key=lambda x: (x[0], x[1]))
        issue_in_start_order([x[2] for x in tasks])
